import numpy as np
import ml_dtypes


def mxq(x, axis, fmt="e4m3"):
    dtype, down = {"e4m3": (ml_dtypes.float8_e4m3fn, 7), "e5m2": (ml_dtypes.float8_e5m2, 14)}[fmt]
    v = np.moveaxis(np.asarray(x, np.float32).astype(ml_dtypes.bfloat16).astype(np.float64), axis, -1)
    blocks = v.reshape(v.shape[:-1] + (-1, 32))
    amax = np.abs(blocks).max(-1, keepdims=True)
    byte = np.maximum(np.where(amax > 0, np.frexp(amax)[1] - 1 + 127, 0) - down, 1)
    scale = np.exp2(byte - 127.0)
    codes = (blocks / scale).astype(np.float32).astype(dtype).astype(np.float64)
    return np.moveaxis((codes * scale).reshape(v.shape), -1, axis)


WIDE = False


def mx_kscale(k):
    if not WIDE:
        return np.ones(k)
    levels = np.array([10, -10, 5, -5, 0])
    if k % 512:
        return np.exp2(np.random.permutation(np.resize(levels, k // 32))).repeat(32)
    a = np.empty((k // 512, 16))
    for p in range(k // 512):
        a[p, :8] = np.random.permutation(np.resize(levels, 8))
        for g in range(8):
            far = levels[np.abs(levels - a[p, g]) >= 10]
            a[p, g + 8] = far[np.random.randint(len(far))]
    return np.exp2(a.ravel()).repeat(32)


def f64(x):
    return np.asarray(x).astype(np.float64)


def striped(idx):
    return np.tile(np.asarray(idx).reshape(-1, 16).T, (8, 1)).astype(np.uint16)


def unstriped(offs):
    return offs[:16].T.reshape(-1).astype(np.int64)


E2M1 = np.array([0.0, 0.5, 1.0, 1.5, 2.0, 3.0, 4.0, 6.0, -0.0, -0.5, -1.0, -1.5, -2.0, -3.0, -4.0, -6.0])


def pack_weight(w, fmt):
    k, n = w.shape
    w = f64(np.asarray(w, np.float32).astype(ml_dtypes.bfloat16)).reshape(k // 32, 32, n)
    amax = np.abs(w).max(1)
    if fmt == "e4m3":
        byte = np.frexp(amax)[1] - 1 + 127 - 7
    else:
        mant, ex = np.frexp(amax / 6.0)
        byte = np.where(mant > 0.5, ex, ex - 1) + 127
    byte = np.clip(np.where(amax > 0, byte, 1), 1, 254)
    scaled = (w * np.exp2(127.0 - byte)[:, None, :]).reshape(k, n).astype(np.float32)
    by_word = np.ascontiguousarray(scaled.reshape(k // 512, 128, 4, n).transpose(0, 1, 3, 2))
    if fmt == "e4m3":
        words = by_word.astype(ml_dtypes.float8_e4m3fn).view(np.uint8)
    else:
        c = by_word.astype(ml_dtypes.float4_e2m1fn).view(np.uint8) & 0xF
        words = (c[..., 0::2] | (c[..., 1::2] << 4)).reshape(k // 512, 128, 2 * n)
    return np.ascontiguousarray(words), np.ascontiguousarray(byte.astype(np.uint8).reshape(k // 512, 16, n))


def unpack_weight(words, scales, fmt):
    g, _, n = scales.shape
    words = np.ascontiguousarray(words).reshape(g, 128, n, -1)
    if fmt == "e4m3":
        vals = words.view(ml_dtypes.float8_e4m3fn).astype(np.float64)
    else:
        nib = np.empty((g, 128, n, 4), np.uint8)
        nib[..., 0::2] = words & 0xF
        nib[..., 1::2] = words >> 4
        vals = E2M1[nib]
    vals = vals * np.repeat(np.exp2(scales.astype(np.float64) - 127.0), 8, axis=1)[..., None]
    return vals.transpose(0, 1, 3, 2).reshape(g * 512, n)


B, N, T, D, DV, NQ = 1, 1024, 2048, 512, 256, 256
CAP = 2.0


def setup_inputs():
    n = np.random.standard_normal
    idx = np.random.permutation(T)[:B * N]
    s = mx_kscale(D)[:, None]
    u = np.ones(T)
    u[idx] = mx_kscale(B * N)
    r = np.random.uniform(0.5, 2.0, T)
    k = n((D, T)) / s
    v = n((DV, T)) / (u * r)
    kp = pack_weight(k, "e4m3")
    return {
        "qT": (n((B, D, NQ)) * s * (1.00 / np.sqrt(D))).astype(np.float32),
        "k_words": kp[0],
        "k_scales": kp[1],
        "vT": v.astype(np.float32),
        "vs": np.tile(u * r, (128, 1)).astype(np.float32),
        "offs": striped(idx),
    }


def reference(qT, k_words, k_scales, vT, vs, offs):
    idx = unstriped(offs)
    k = unpack_weight(k_words, k_scales, "e4m3")
    v = f64(vT)
    pick = lambda x: x[:, idx].reshape(x.shape[0], B, N).transpose(1, 0, 2)
    q = f64(qT)
    score = mxq(q, 1, "e4m3").transpose(0, 2, 1) @ pick(k)
    score = CAP * np.tanh(score / CAP)
    m = score.max(-1, keepdims=True)
    p = np.exp(score - m)
    total = p.sum(-1, keepdims=True)
    w = p * pick(f64(vs))[:, :1, :]
    y = mxq(w, 2, "e4m3") @ mxq(pick(v).transpose(0, 2, 1), 1, "e4m3")
    y = y / total
    return y

@@ -1,0 +1,166 @@
+from contextlib import ExitStack
+
+import concourse.mybir as mybir
+from concourse.masks import make_identity
+
+F32 = mybir.dt.float32
+BF16 = mybir.dt.bfloat16
+I32 = mybir.dt.int32
+U32 = mybir.dt.uint32
+U16 = mybir.dt.uint16
+U8 = mybir.dt.uint8
+FP8X4 = mybir.dt.float8_e4m3fn_x4
+ACT = mybir.ActivationFunctionType
+ALU = mybir.AluOpType
+
+P = 128
+T, N, D, DV, NQ = 2048, 1024, 512, 256, 256
+CAP = 2.0
+FLOPS = 2 * NQ * N * (D + DV)
+BYTES = 4 * D * NQ + D * T + 16 * T + 4 * DV * T + 4 * T + 2 * P * N // 16 + 4 * NQ * DV
+
+
+def tile_attend_cap_topk_kernel(tc, qT, k_words, k_scales, vT, vs, offs, out):
+    nc = tc.nc
+    with ExitStack() as ctx:
+        sb = ctx.enter_context(tc.tile_pool(name="sb", bufs=1))
+        ps = ctx.enter_context(tc.psum_pool(name="ps", bufs=1))
+
+        offsets = sb.tile([P, N // 16], U16, name="offsets")
+        ks_pool = sb.tile([P, T], U8, name="ks_pool", align_bytes=64)
+        kw_pool = sb.tile([P, T], U32, name="kw_pool", align_bytes=64)
+        vs_pool = sb.tile([P, T], F32, name="vs_pool", align_bytes=64)
+        q_raw = sb.tile([P, 4, NQ], F32, name="q_raw", align_bytes=64)
+        v0_raw = [sb.tile([P, T // 2], F32, name="v0_raw%d" % c, align_bytes=64) for c in range(2)]
+        v0_pool = sb.tile([P, T], BF16, name="v0_pool", align_bytes=64)
+        v1_pool = sb.tile([P, T], F32, name="v1_pool", align_bytes=64)
+        ident = sb.tile([P, P], F32, name="ident", align_bytes=64)
+        warm = sb.tile([P, 1], F32, name="warm")
+        warm2 = sb.tile([P, 1], F32, name="warm2")
+
+        nc.vector.memset(warm[:], 0.0)
+        nc.vector.memset(vs_pool[:, 0 : T // 2], 0.0)
+        nc.gpsimd.memset(vs_pool[:, T // 2 : T], 0.0)
+        nc.scalar.activation(warm2[:], warm[:], ACT.Exp)
+        make_identity(nc, ident[:])
+
+        nc.sync.dma_start(offsets[:], offs)
+        for quad in range(4):
+            nc.sync.dma_start(ks_pool[32 * quad : 32 * quad + 32, :].bitcast(I32), k_scales[0:1, 4 * quad : 4 * quad + 4, :].bitcast(I32).broadcast_to([8, 4, T // 4]))
+        nc.sync.dma_start(q_raw[:], qT[0].rearrange("(p j) q -> p j q", j=4))
+        nc.sync.dma_start(v0_raw[0][:], vT[0:P, 0 : T // 2])
+        nc.sync.dma_start(v0_raw[1][:], vT[0:P, T // 2 : T])
+        nc.sync.dma_start(vs_pool[0:1, :], vs[0:1, :])
+        nc.sync.dma_start(kw_pool[:].bitcast(I32), k_words[0].rearrange("p t r -> p (t r)").bitcast(I32))
+        nc.sync.dma_start(v1_pool[:], vT[P : 2 * P, :])
+
+        q_b = sb.tile([P, NQ, 4], BF16, name="q_b", align_bytes=64)
+        nc.scalar.copy(q_b[:], q_raw[:].rearrange("p j q -> p q j"))
+        q_codes = sb.tile([P, NQ], U32, name="q_codes", align_bytes=64)
+        q_scales = sb.tile([P, NQ], U8, name="q_scales", align_bytes=64)
+
+        ks_g = sb.tile([P, N], U8, name="ks_g", align_bytes=64)
+        kw_g = sb.tile([P, N], U32, name="kw_g", align_bytes=64)
+        vs_g = sb.tile([P, N], F32, name="vs_g", align_bytes=64)
+        v_g = [sb.tile([P, N], BF16, name="v_g%d" % e, align_bytes=64) for e in range(2)]
+
+        nc.vector.tensor_copy(ks_g[:], ks_pool[:].indirect(offsets[:]))
+        nc.vector.tensor_copy(vs_g[:], vs_pool[:].indirect(offsets[:]))
+        nc.vector.quantize_mx(q_codes[:].bitcast(FP8X4), q_scales[:], q_b[:].rearrange("p q j -> p (q j)"))
+        for g in range(2):
+            nc.vector.tensor_copy(kw_g[:, 512 * g : 512 * (g + 1)], kw_pool[:].indirect(offsets[:, 32 * g : 32 * (g + 1)]))
+
+
+        for c in range(2):
+            nc.scalar.activation(v0_pool[:, c * (T // 2) : (c + 1) * (T // 2)], v0_raw[c][:], ACT.Copy)
+        nc.scalar.activation(v_g[0][:], v0_pool[:].indirect(offsets[:]), ACT.Copy)
+
+        vs_col = sb.tile([P, 2, 4], F32, name="vs_col")
+        for g in range(2):
+            turn = ps.tile([P, 4, P], F32, name="vs_turn", tag="side%d" % g)
+            for t in range(4):
+                nc.tensor.transpose(turn[:, t, :], vs_g[:, 512 * g + t : 512 * (g + 1) : 4], ident[:])
+            nc.scalar.copy(vs_col[:, g, :], turn[:, :, 0])
+
+        th = [sb.tile([P, 2, 4, P], F32, name="th%d" % a, tag="th%d" % a, align_bytes=64) for a in range(2)]
+        for a, g in ((0, 0), (0, 1), (1, 0), (1, 1)):
+            score = ps.tile([P, 512], F32, name="score", tag="main%d" % (2 * a + g))
+            nc.tensor.matmul_mx(
+                score[:],
+                lhsT=q_codes[:, a * P : (a + 1) * P].bitcast(FP8X4),
+                lhsT_scale=q_scales[:, a * P : (a + 1) * P],
+                rhs=kw_g[:, 512 * g : 512 * (g + 1)].bitcast(FP8X4),
+                rhs_scale=ks_g[:, 512 * g : 512 * (g + 1)],
+                start=True,
+                stop=True,
+            )
+            nc.scalar.activation(th[a][:, g, :, :], score[:].rearrange("q (s t) -> q t s", t=4), ACT.Tanh, scale=1.0 / CAP)
+
+        nc.vector.tensor_copy(v_g[1][:], v1_pool[:].indirect(offsets[:]))
+
+        neg_c = [sb.tile([P, N], F32, name="neg_c%d" % a) for a in range(2)]
+        neg_m = [sb.tile([P, 1], F32, name="neg_m%d" % a) for a in range(2)]
+        prob = [sb.tile([P, 2, 4, P], F32, name="prob%d" % a) for a in range(2)]
+        total = sb.tile([P, 2], F32, name="total")
+        for a in range(2):
+            nc.vector.tensor_scalar(neg_c[a][:], th[a][:].rearrange("q g t s -> q (g t s)"), -CAP, None, ALU.mult, ALU.min, accum_out=neg_m[a][:])
+            nc.scalar.activation(prob[a][:].rearrange("q g t s -> q (g t s)"), neg_c[a][:], ACT.Exp, bias=neg_m[a][:], scale=-1.0, accum_out=total[:, a : a + 1])
+
+        v_b = sb.tile([P, 2, DV, 4], BF16, name="v_b", align_bytes=64)
+        v_words = v_b[:].rearrange("p g e t -> p (g e t)").bitcast(F32).rearrange("p (g e u) -> p g e u", g=2, u=2)
+        for e in range(2):
+            words = v_g[e][:].bitcast(F32)
+            turn = ps.tile([P, 2, 2, P], F32, name="v_turn", tag="main%d" % (2 + e))
+            for g in range(2):
+                for u in range(2):
+                    nc.tensor.transpose(turn[:, g, u, :], words[:, 256 * g + u : 256 * (g + 1) : 2], ident[:])
+            nc.scalar.copy(v_words[:, :, e * P : (e + 1) * P, :], turn[:].rearrange("p g u e -> p g e u"))
+        v_codes = sb.tile([P, 2, DV], U32, name="v_codes", tag="th1", align_bytes=64)
+        v_scales = sb.tile([P, 2, DV], U8, name="v_scales", align_bytes=64)
+        nc.vector.quantize_mx(v_codes[:].rearrange("p g e -> p (g e)").bitcast(FP8X4), v_scales[:].rearrange("p g e -> p (g e)"), v_b[:].rearrange("p g e t -> p (g e t)"))
+
+        inv = sb.tile([P, 2], F32, name="inv")
+        nc.vector.reciprocal(inv[:], total[:])
+
+        w_b = {}
+        w_codes = {}
+        w_scales = {}
+
+        def weigh(a, g):
+            turn = ps.tile([P, 4, P], F32, name="p_turn", tag=("main%d", "side%d")[a] % g)
+            for t in range(4):
+                nc.tensor.transpose(turn[:, t, :], prob[a][:, g, t, :], ident[:])
+            w_b[a, g] = sb.tile([P, P, 4], BF16, name="w_b%d%d" % (a, g), align_bytes=64)
+            nc.vector.tensor_tensor(w_b[a, g][:], turn[:].rearrange("s t q -> s q t"), vs_col[:, g : g + 1, :].broadcast_to([P, P, 4]), ALU.mult)
+
+        def quant(a, g):
+            w_codes[a, g] = sb.tile([P, P], U32, name="w_codes%d%d" % (a, g), align_bytes=64)
+            w_scales[a, g] = sb.tile([P, P], U8, name="w_scales%d%d" % (a, g), align_bytes=64)
+            nc.vector.quantize_mx(w_codes[a, g][:].bitcast(FP8X4), w_scales[a, g][:], w_b[a, g][:].rearrange("s q t -> s (q t)"))
+
+        def finish(a):
+            y = ps.tile([P, DV], F32, name="y", tag="y%d" % a)
+            for g in range(2):
+                nc.tensor.matmul_mx(
+                    y[:],
+                    lhsT=w_codes[a, g][:].bitcast(FP8X4),
+                    lhsT_scale=w_scales[a, g][:],
+                    rhs=v_codes[:, g, :].bitcast(FP8X4),
+                    rhs_scale=v_scales[:, g, :],
+                    start=(g == 0),
+                    stop=(g == 1),
+                )
+            res = sb.tile([P, DV], F32, name="res%d" % a)
+            nc.scalar.activation(res[:], y[:], ACT.Copy, scale=inv[:, a : a + 1])
+            nc.sync.dma_start(out[0, a * P : (a + 1) * P, :], res[:])
+
+        weigh(0, 0)
+        weigh(0, 1)
+        quant(0, 0)
+        weigh(1, 0)
+        quant(0, 1)
+        finish(0)
+        weigh(1, 1)
+        quant(1, 0)
+        quant(1, 1)
+        finish(1)

@@ -33,7 +33,7 @@ def tile_attend_cap_topk_kernel(tc, qT, k_words, k_scales, vT, vs, offs, out):
         q_raw = sb.tile([P, 4, NQ], F32, name="q_raw", align_bytes=64)
         v0_raw = [sb.tile([P, T // 2], F32, name="v0_raw%d" % c, align_bytes=64) for c in range(2)]
         v0_pool = sb.tile([P, T], BF16, name="v0_pool", align_bytes=64)
-        v1_pool = sb.tile([P, T], F32, name="v1_pool", align_bytes=64)
+        v1_pool = sb.tile([P, T], F32, name="v1_pool", tag="v1_pool", align_bytes=64)
         ident = sb.tile([P, P], F32, name="ident", align_bytes=64)
         warm = sb.tile([P, 1], F32, name="warm")
         warm2 = sb.tile([P, 1], F32, name="warm2")
@@ -75,12 +75,9 @@ def tile_attend_cap_topk_kernel(tc, qT, k_words, k_scales, vT, vs, offs, out):
             nc.scalar.activation(v0_pool[:, c * (T // 2) : (c + 1) * (T // 2)], v0_raw[c][:], ACT.Copy)
         nc.scalar.activation(v_g[0][:], v0_pool[:].indirect(offsets[:]), ACT.Copy)
 
-        vs_col = sb.tile([P, 2, 4], F32, name="vs_col")
+        vs_col = [sb.tile([P, 4], F32, name="vs_col%d" % g) for g in range(2)]
         for g in range(2):
-            turn = ps.tile([P, 4, P], F32, name="vs_turn", tag="side%d" % g)
-            for t in range(4):
-                nc.tensor.transpose(turn[:, t, :], vs_g[:, 512 * g + t : 512 * (g + 1) : 4], ident[:])
-            nc.scalar.copy(vs_col[:, g, :], turn[:, :, 0])
+            nc.sync.dma_start(vs_col[g][:], vs_g[0:1, 512 * g : 512 * (g + 1)])
 
         th = [sb.tile([P, 2, 4, P], F32, name="th%d" % a, tag="th%d" % a, align_bytes=64) for a in range(2)]
         for a, g in ((0, 0), (0, 1), (1, 0), (1, 1)):
@@ -98,13 +95,13 @@ def tile_attend_cap_topk_kernel(tc, qT, k_words, k_scales, vT, vs, offs, out):
 
         nc.vector.tensor_copy(v_g[1][:], v1_pool[:].indirect(offsets[:]))
 
-        neg_c = [sb.tile([P, N], F32, name="neg_c%d" % a) for a in range(2)]
+        neg_c = sb.tile([P, 2, N], F32, name="neg_c", tag="v1_pool", align_bytes=64)
         neg_m = [sb.tile([P, 1], F32, name="neg_m%d" % a) for a in range(2)]
         prob = [sb.tile([P, 2, 4, P], F32, name="prob%d" % a) for a in range(2)]
         total = sb.tile([P, 2], F32, name="total")
         for a in range(2):
-            nc.vector.tensor_scalar(neg_c[a][:], th[a][:].rearrange("q g t s -> q (g t s)"), -CAP, None, ALU.mult, ALU.min, accum_out=neg_m[a][:])
-            nc.scalar.activation(prob[a][:].rearrange("q g t s -> q (g t s)"), neg_c[a][:], ACT.Exp, bias=neg_m[a][:], scale=-1.0, accum_out=total[:, a : a + 1])
+            nc.vector.tensor_scalar(neg_c[:, a, :], th[a][:].rearrange("q g t s -> q (g t s)"), -CAP, None, ALU.mult, ALU.min, accum_out=neg_m[a][:])
+            nc.scalar.activation(prob[a][:].rearrange("q g t s -> q (g t s)"), neg_c[:, a, :], ACT.Exp, bias=neg_m[a][:], scale=-1.0, accum_out=total[:, a : a + 1])
 
         v_b = sb.tile([P, 2, DV, 4], BF16, name="v_b", align_bytes=64)
         v_words = v_b[:].rearrange("p g e t -> p (g e t)").bitcast(F32).rearrange("p (g e u) -> p g e u", g=2, u=2)
@@ -131,7 +128,7 @@ def tile_attend_cap_topk_kernel(tc, qT, k_words, k_scales, vT, vs, offs, out):
             for t in range(4):
                 nc.tensor.transpose(turn[:, t, :], prob[a][:, g, t, :], ident[:])
             w_b[a, g] = sb.tile([P, P, 4], BF16, name="w_b%d%d" % (a, g), align_bytes=64)
-            nc.vector.tensor_tensor(w_b[a, g][:], turn[:].rearrange("s t q -> s q t"), vs_col[:, g : g + 1, :].broadcast_to([P, P, 4]), ALU.mult)
+            nc.vector.tensor_tensor(w_b[a, g][:], turn[:].rearrange("s t q -> s q t"), vs_col[g][:].unsqueeze(1).broadcast_to([P, P, 4]), ALU.mult)
 
         def quant(a, g):
             w_codes[a, g] = sb.tile([P, P], U32, name="w_codes%d%d" % (a, g), align_bytes=64)

@@ -44,13 +44,15 @@ def tile_attend_cap_topk_kernel(tc, qT, k_words, k_scales, vT, vs, offs, out):
         nc.scalar.activation(warm2[:], warm[:], ACT.Exp)
         make_identity(nc, ident[:])
 
-        nc.sync.dma_start(offsets[:], offs)
         for quad in range(4):
             nc.sync.dma_start(ks_pool[32 * quad : 32 * quad + 32, :].bitcast(I32), k_scales[0:1, 4 * quad : 4 * quad + 4, :].bitcast(I32).broadcast_to([8, 4, T // 4]))
+        nc.sync.dma_start(offsets[:], offs)
+        for quad in range(4, 4):
+            nc.sync.dma_start(ks_pool[32 * quad : 32 * quad + 4, :].bitcast(I32), k_scales[0, 4 * quad : 4 * quad + 4, :].bitcast(I32))
         nc.sync.dma_start(q_raw[:], qT[0].rearrange("(p j) q -> p j q", j=4))
+        nc.sync.dma_start(vs_pool[0:1, :], vs[0:1, :])
         nc.sync.dma_start(v0_raw[0][:], vT[0:P, 0 : T // 2])
         nc.sync.dma_start(v0_raw[1][:], vT[0:P, T // 2 : T])
-        nc.sync.dma_start(vs_pool[0:1, :], vs[0:1, :])
         nc.sync.dma_start(kw_pool[:].bitcast(I32), k_words[0].rearrange("p t r -> p (t r)").bitcast(I32))
         nc.sync.dma_start(v1_pool[:], vT[P : 2 * P, :])
 
@@ -93,15 +95,18 @@ def tile_attend_cap_topk_kernel(tc, qT, k_words, k_scales, vT, vs, offs, out):
             )
             nc.scalar.activation(th[a][:, g, :, :], score[:].rearrange("q (s t) -> q t s", t=4), ACT.Tanh, scale=1.0 / CAP)
 
-        nc.vector.tensor_copy(v_g[1][:], v1_pool[:].indirect(offsets[:]))
+        for g in range(2):
+            nc.vector.tensor_copy(v_g[1][:, 512 * g : 512 * (g + 1)], v1_pool[:].indirect(offsets[:, 32 * g : 32 * (g + 1)]))
 
         neg_c = sb.tile([P, 2, N], F32, name="neg_c", tag="v1_pool", align_bytes=64)
         neg_m = [sb.tile([P, 1], F32, name="neg_m%d" % a) for a in range(2)]
         prob = [sb.tile([P, 2, 4, P], F32, name="prob%d" % a) for a in range(2)]
+        part = sb.tile([P, 2, 2], F32, name="part")
         total = sb.tile([P, 2], F32, name="total")
         for a in range(2):
             nc.vector.tensor_scalar(neg_c[:, a, :], th[a][:].rearrange("q g t s -> q (g t s)"), -CAP, None, ALU.mult, ALU.min, accum_out=neg_m[a][:])
-            nc.scalar.activation(prob[a][:].rearrange("q g t s -> q (g t s)"), neg_c[:, a, :], ACT.Exp, bias=neg_m[a][:], scale=-1.0, accum_out=total[:, a : a + 1])
+            for g in range(2):
+                nc.scalar.activation(prob[a][:, g, :, :].rearrange("q t s -> q (t s)"), neg_c[:, a, 512 * g : 512 * (g + 1)], ACT.Exp, bias=neg_m[a][:], scale=-1.0, accum_out=part[:, a, g : g + 1])
 
         v_b = sb.tile([P, 2, DV, 4], BF16, name="v_b", align_bytes=64)
         v_words = v_b[:].rearrange("p g e t -> p (g e t)").bitcast(F32).rearrange("p (g e u) -> p g e u", g=2, u=2)
@@ -117,6 +122,7 @@ def tile_attend_cap_topk_kernel(tc, qT, k_words, k_scales, vT, vs, offs, out):
         nc.vector.quantize_mx(v_codes[:].rearrange("p g e -> p (g e)").bitcast(FP8X4), v_scales[:].rearrange("p g e -> p (g e)"), v_b[:].rearrange("p g e t -> p (g e t)"))
 
         inv = sb.tile([P, 2], F32, name="inv")
+        nc.gpsimd.tensor_tensor(total[:], part[:, :, 0], part[:, :, 1], ALU.add)
         nc.vector.reciprocal(inv[:], total[:])
 
         w_b = {}
@@ -135,29 +141,35 @@ def tile_attend_cap_topk_kernel(tc, qT, k_words, k_scales, vT, vs, offs, out):
             w_scales[a, g] = sb.tile([P, P], U8, name="w_scales%d%d" % (a, g), align_bytes=64)
             nc.vector.quantize_mx(w_codes[a, g][:].bitcast(FP8X4), w_scales[a, g][:], w_b[a, g][:].rearrange("s q t -> s (q t)"))
 
-        def finish(a):
-            y = ps.tile([P, DV], F32, name="y", tag="y%d" % a)
+        def finish(a, cols, tag, on_vector):
+            width = cols.stop - cols.start
+            y = ps.tile([P, width], F32, name="y", tag=tag)
             for g in range(2):
                 nc.tensor.matmul_mx(
                     y[:],
                     lhsT=w_codes[a, g][:].bitcast(FP8X4),
                     lhsT_scale=w_scales[a, g][:],
-                    rhs=v_codes[:, g, :].bitcast(FP8X4),
-                    rhs_scale=v_scales[:, g, :],
+                    rhs=v_codes[:, g, cols].bitcast(FP8X4),
+                    rhs_scale=v_scales[:, g, cols],
                     start=(g == 0),
                     stop=(g == 1),
                 )
-            res = sb.tile([P, DV], F32, name="res%d" % a)
-            nc.scalar.activation(res[:], y[:], ACT.Copy, scale=inv[:, a : a + 1])
-            nc.sync.dma_start(out[0, a * P : (a + 1) * P, :], res[:])
+            res = sb.tile([P, width], F32, name="res" + tag)
+            if on_vector:
+                nc.vector.tensor_scalar(res[:], y[:], inv[:, a : a + 1], None, ALU.mult)
+                nc.sync.dma_start(out[0, a * P : (a + 1) * P, cols], res[:])
+            else:
+                nc.scalar.activation(res[:], y[:], ACT.Copy, scale=inv[:, a : a + 1])
+                (nc.sync, nc.scalar)[a].dma_start(out[0, a * P : (a + 1) * P, cols], res[:])
 
         weigh(0, 0)
         weigh(0, 1)
         quant(0, 0)
         weigh(1, 0)
         quant(0, 1)
-        finish(0)
+        finish(0, slice(0, DV), "y0", False)
         weigh(1, 1)
         quant(1, 0)
         quant(1, 1)
-        finish(1)
+        finish(1, slice(0, P), "y1", False)
+        finish(1, slice(P, DV), "main2", True)

@@ -14,10 +14,17 @@ ACT = mybir.ActivationFunctionType
 ALU = mybir.AluOpType
 
 P = 128
+PACK = 4
+PASS = P * PACK
 T, N, D, DV, NQ = 2048, 1024, 512, 256, 256
+PASSES = N // PASS
+Q_TILES = NQ // P
+LIST_COLS = PASS // 16
+QUADRANT = 32
 CAP = 2.0
+
 FLOPS = 2 * NQ * N * (D + DV)
-BYTES = 4 * D * NQ + D * T + 16 * T + 4 * DV * T + 4 * T + 2 * P * N // 16 + 4 * NQ * DV
+BYTES = 4 * D * NQ + D * T + (D // 32) * T + 4 * DV * T + 4 * T + 2 * P * N // 16 + 4 * NQ * DV
 
 
 def tile_attend_cap_topk_kernel(tc, qT, k_words, k_scales, vT, vs, offs, out):
@@ -26,102 +33,120 @@ def tile_attend_cap_topk_kernel(tc, qT, k_words, k_scales, vT, vs, offs, out):
         sb = ctx.enter_context(tc.tile_pool(name="sb", bufs=1))
         ps = ctx.enter_context(tc.psum_pool(name="ps", bufs=1))
 
+
         offsets = sb.tile([P, N // 16], U16, name="offsets")
         ks_pool = sb.tile([P, T], U8, name="ks_pool", align_bytes=64)
         kw_pool = sb.tile([P, T], U32, name="kw_pool", align_bytes=64)
         vs_pool = sb.tile([P, T], F32, name="vs_pool", align_bytes=64)
-        q_raw = sb.tile([P, 4, NQ], F32, name="q_raw", align_bytes=64)
+        q_raw = sb.tile([P, PACK, NQ], F32, name="q_raw", align_bytes=64)
         v0_raw = [sb.tile([P, T // 2], F32, name="v0_raw%d" % c, align_bytes=64) for c in range(2)]
         v0_pool = sb.tile([P, T], BF16, name="v0_pool", align_bytes=64)
         v1_pool = sb.tile([P, T], F32, name="v1_pool", tag="v1_pool", align_bytes=64)
         ident = sb.tile([P, P], F32, name="ident", align_bytes=64)
-        warm = sb.tile([P, 1], F32, name="warm")
-        warm2 = sb.tile([P, 1], F32, name="warm2")
 
-        nc.vector.memset(warm[:], 0.0)
         nc.vector.memset(vs_pool[:, 0 : T // 2], 0.0)
         nc.gpsimd.memset(vs_pool[:, T // 2 : T], 0.0)
-        nc.scalar.activation(warm2[:], warm[:], ACT.Exp)
         make_identity(nc, ident[:])
 
-        for quad in range(4):
-            nc.sync.dma_start(ks_pool[32 * quad : 32 * quad + 32, :].bitcast(I32), k_scales[0:1, 4 * quad : 4 * quad + 4, :].bitcast(I32).broadcast_to([8, 4, T // 4]))
+        for quad in range(P // QUADRANT):
+            rows = k_scales[0:1, 4 * quad : 4 * quad + 4, :].bitcast(I32)
+            nc.sync.dma_start(
+                ks_pool[QUADRANT * quad : QUADRANT * (quad + 1), :].bitcast(I32),
+                rows.broadcast_to([QUADRANT // 4, 4, T // 4]),
+            )
         nc.sync.dma_start(offsets[:], offs)
-        for quad in range(4, 4):
-            nc.sync.dma_start(ks_pool[32 * quad : 32 * quad + 4, :].bitcast(I32), k_scales[0, 4 * quad : 4 * quad + 4, :].bitcast(I32))
-        nc.sync.dma_start(q_raw[:], qT[0].rearrange("(p j) q -> p j q", j=4))
+        nc.sync.dma_start(q_raw[:], qT[0].rearrange("(p j) q -> p j q", j=PACK))
         nc.sync.dma_start(vs_pool[0:1, :], vs[0:1, :])
-        nc.sync.dma_start(v0_raw[0][:], vT[0:P, 0 : T // 2])
-        nc.sync.dma_start(v0_raw[1][:], vT[0:P, T // 2 : T])
+        for c in range(2):
+            nc.sync.dma_start(v0_raw[c][:], vT[0:P, c * (T // 2) : (c + 1) * (T // 2)])
         nc.sync.dma_start(kw_pool[:].bitcast(I32), k_words[0].rearrange("p t r -> p (t r)").bitcast(I32))
         nc.sync.dma_start(v1_pool[:], vT[P : 2 * P, :])
 
-        q_b = sb.tile([P, NQ, 4], BF16, name="q_b", align_bytes=64)
-        nc.scalar.copy(q_b[:], q_raw[:].rearrange("p j q -> p q j"))
+        q_b = sb.tile([P, NQ, PACK], BF16, name="q_b", align_bytes=64)
+        nc.scalar.activation(q_b[:], q_raw[:].rearrange("p j q -> p q j"), ACT.Copy)
         q_codes = sb.tile([P, NQ], U32, name="q_codes", align_bytes=64)
         q_scales = sb.tile([P, NQ], U8, name="q_scales", align_bytes=64)
 
         ks_g = sb.tile([P, N], U8, name="ks_g", align_bytes=64)
         kw_g = sb.tile([P, N], U32, name="kw_g", align_bytes=64)
         vs_g = sb.tile([P, N], F32, name="vs_g", align_bytes=64)
-        v_g = [sb.tile([P, N], BF16, name="v_g%d" % e, align_bytes=64) for e in range(2)]
+        v_g = [sb.tile([P, N], BF16, name="v_g%d" % e, align_bytes=64) for e in range(DV // P)]
+
+        def slots(g):
+            return slice(PASS * g, PASS * (g + 1))
+
+        def entries(g):
+            return offsets[:, LIST_COLS * g : LIST_COLS * (g + 1)]
 
         nc.vector.tensor_copy(ks_g[:], ks_pool[:].indirect(offsets[:]))
         nc.vector.tensor_copy(vs_g[:], vs_pool[:].indirect(offsets[:]))
         nc.vector.quantize_mx(q_codes[:].bitcast(FP8X4), q_scales[:], q_b[:].rearrange("p q j -> p (q j)"))
-        for g in range(2):
-            nc.vector.tensor_copy(kw_g[:, 512 * g : 512 * (g + 1)], kw_pool[:].indirect(offsets[:, 32 * g : 32 * (g + 1)]))
-
+        for g in range(PASSES):
+            nc.vector.tensor_copy(kw_g[:, slots(g)], kw_pool[:].indirect(entries(g)))
 
         for c in range(2):
             nc.scalar.activation(v0_pool[:, c * (T // 2) : (c + 1) * (T // 2)], v0_raw[c][:], ACT.Copy)
         nc.scalar.activation(v_g[0][:], v0_pool[:].indirect(offsets[:]), ACT.Copy)
 
-        vs_col = [sb.tile([P, 4], F32, name="vs_col%d" % g) for g in range(2)]
-        for g in range(2):
-            nc.sync.dma_start(vs_col[g][:], vs_g[0:1, 512 * g : 512 * (g + 1)])
+        vs_col = [sb.tile([P, PACK], F32, name="vs_col%d" % g) for g in range(PASSES)]
+        for g in range(PASSES):
+            nc.sync.dma_start(vs_col[g][:], vs_g[0:1, slots(g)])
 
-        th = [sb.tile([P, 2, 4, P], F32, name="th%d" % a, tag="th%d" % a, align_bytes=64) for a in range(2)]
-        for a, g in ((0, 0), (0, 1), (1, 0), (1, 1)):
-            score = ps.tile([P, 512], F32, name="score", tag="main%d" % (2 * a + g))
-            nc.tensor.matmul_mx(
-                score[:],
-                lhsT=q_codes[:, a * P : (a + 1) * P].bitcast(FP8X4),
-                lhsT_scale=q_scales[:, a * P : (a + 1) * P],
-                rhs=kw_g[:, 512 * g : 512 * (g + 1)].bitcast(FP8X4),
-                rhs_scale=ks_g[:, 512 * g : 512 * (g + 1)],
-                start=True,
-                stop=True,
+        th = [sb.tile([P, PASSES, PACK, P], F32, name="th%d" % a, tag="th%d" % a, align_bytes=64) for a in range(Q_TILES)]
+        for a in range(Q_TILES):
+            for g in range(PASSES):
+                score = ps.tile([P, PASS], F32, name="score", tag="score%d" % (PASSES * a + g))
+                nc.tensor.matmul_mx(
+                    score[:],
+                    lhsT=q_codes[:, a * P : (a + 1) * P].bitcast(FP8X4),
+                    lhsT_scale=q_scales[:, a * P : (a + 1) * P],
+                    rhs=kw_g[:, slots(g)].bitcast(FP8X4),
+                    rhs_scale=ks_g[:, slots(g)],
+                    start=True,
+                    stop=True,
+                )
+                nc.scalar.activation(th[a][:, g, :, :], score[:].rearrange("q (s t) -> q t s", t=PACK), ACT.Tanh, scale=1.0 / CAP)
+
+        for g in range(PASSES):
+            nc.vector.tensor_copy(v_g[1][:, slots(g)], v1_pool[:].indirect(entries(g)))
+
+        neg_c = sb.tile([P, Q_TILES, N], F32, name="neg_c", tag="v1_pool", align_bytes=64)
+        neg_m = [sb.tile([P, 1], F32, name="neg_m%d" % a) for a in range(Q_TILES)]
+        prob = [sb.tile([P, PASSES, PACK, P], F32, name="prob%d" % a) for a in range(Q_TILES)]
+        part = sb.tile([P, Q_TILES, PASSES], F32, name="part")
+        total = sb.tile([P, Q_TILES], F32, name="total")
+        for a in range(Q_TILES):
+            nc.vector.tensor_scalar(
+                neg_c[:, a, :], th[a][:].rearrange("q g t s -> q (g t s)"), -CAP, None, ALU.mult, ALU.min, accum_out=neg_m[a][:]
             )
-            nc.scalar.activation(th[a][:, g, :, :], score[:].rearrange("q (s t) -> q t s", t=4), ACT.Tanh, scale=1.0 / CAP)
+            for g in range(PASSES):
+                nc.scalar.activation(
+                    prob[a][:, g, :, :].rearrange("q t s -> q (t s)"),
+                    neg_c[:, a, slots(g)],
+                    ACT.Exp,
+                    bias=neg_m[a][:],
+                    scale=-1.0,
+                    accum_out=part[:, a, g : g + 1],
+                )
 
-        for g in range(2):
-            nc.vector.tensor_copy(v_g[1][:, 512 * g : 512 * (g + 1)], v1_pool[:].indirect(offsets[:, 32 * g : 32 * (g + 1)]))
-
-        neg_c = sb.tile([P, 2, N], F32, name="neg_c", tag="v1_pool", align_bytes=64)
-        neg_m = [sb.tile([P, 1], F32, name="neg_m%d" % a) for a in range(2)]
-        prob = [sb.tile([P, 2, 4, P], F32, name="prob%d" % a) for a in range(2)]
-        part = sb.tile([P, 2, 2], F32, name="part")
-        total = sb.tile([P, 2], F32, name="total")
-        for a in range(2):
-            nc.vector.tensor_scalar(neg_c[:, a, :], th[a][:].rearrange("q g t s -> q (g t s)"), -CAP, None, ALU.mult, ALU.min, accum_out=neg_m[a][:])
-            for g in range(2):
-                nc.scalar.activation(prob[a][:, g, :, :].rearrange("q t s -> q (t s)"), neg_c[:, a, 512 * g : 512 * (g + 1)], ACT.Exp, bias=neg_m[a][:], scale=-1.0, accum_out=part[:, a, g : g + 1])
-
-        v_b = sb.tile([P, 2, DV, 4], BF16, name="v_b", align_bytes=64)
-        v_words = v_b[:].rearrange("p g e t -> p (g e t)").bitcast(F32).rearrange("p (g e u) -> p g e u", g=2, u=2)
-        for e in range(2):
+        v_b = sb.tile([P, PASSES, DV, PACK], BF16, name="v_b", align_bytes=64)
+        v_words = v_b[:].rearrange("s g e t -> s (g e t)").bitcast(F32).rearrange("s (g e u) -> s g e u", g=PASSES, u=2)
+        for e, passes, bank in ((0, (0, 1), "score2"), (1, (0,), "score3"), (1, (1,), "y1")):
             words = v_g[e][:].bitcast(F32)
-            turn = ps.tile([P, 2, 2, P], F32, name="v_turn", tag="main%d" % (2 + e))
-            for g in range(2):
+            v_turn = ps.tile([P, len(passes), 2, P], F32, name="v_turn", tag=bank)
+            for n, g in enumerate(passes):
                 for u in range(2):
-                    nc.tensor.transpose(turn[:, g, u, :], words[:, 256 * g + u : 256 * (g + 1) : 2], ident[:])
-            nc.scalar.copy(v_words[:, :, e * P : (e + 1) * P, :], turn[:].rearrange("p g u e -> p g e u"))
-        v_codes = sb.tile([P, 2, DV], U32, name="v_codes", tag="th1", align_bytes=64)
-        v_scales = sb.tile([P, 2, DV], U8, name="v_scales", align_bytes=64)
-        nc.vector.quantize_mx(v_codes[:].rearrange("p g e -> p (g e)").bitcast(FP8X4), v_scales[:].rearrange("p g e -> p (g e)"), v_b[:].rearrange("p g e t -> p (g e t)"))
+                    nc.tensor.transpose(v_turn[:, n, u, :], words[:, PASS // 2 * g + u : PASS // 2 * (g + 1) : 2], ident[:])
+            nc.scalar.copy(v_words[:, passes[0] : passes[-1] + 1, e * P : (e + 1) * P, :], v_turn[:].rearrange("s g u e -> s g e u"))
+        v_codes = sb.tile([P, PASSES, DV], U32, name="v_codes", tag="th1", align_bytes=64)
+        v_scales = sb.tile([P, PASSES, DV], U8, name="v_scales", align_bytes=64)
+        nc.vector.quantize_mx(
+            v_codes[:].rearrange("s g e -> s (g e)").bitcast(FP8X4),
+            v_scales[:].rearrange("s g e -> s (g e)"),
+            v_b[:].rearrange("s g e t -> s (g e t)"),
+        )
 
-        inv = sb.tile([P, 2], F32, name="inv")
+        inv = sb.tile([P, Q_TILES], F32, name="inv")
         nc.gpsimd.tensor_tensor(total[:], part[:, :, 0], part[:, :, 1], ALU.add)
         nc.vector.reciprocal(inv[:], total[:])
 
@@ -130,21 +155,22 @@ def tile_attend_cap_topk_kernel(tc, qT, k_words, k_scales, vT, vs, offs, out):
         w_scales = {}
 
         def weigh(a, g):
-            turn = ps.tile([P, 4, P], F32, name="p_turn", tag=("main%d", "side%d")[a] % g)
-            for t in range(4):
-                nc.tensor.transpose(turn[:, t, :], prob[a][:, g, t, :], ident[:])
-            w_b[a, g] = sb.tile([P, P, 4], BF16, name="w_b%d%d" % (a, g), align_bytes=64)
-            nc.vector.tensor_tensor(w_b[a, g][:], turn[:].rearrange("s t q -> s q t"), vs_col[g][:].unsqueeze(1).broadcast_to([P, P, 4]), ALU.mult)
+            p_turn = ps.tile([P, PACK, P], F32, name="p_turn", tag=("score%d", "turn%d")[a] % g)
+            for t in range(PACK):
+                nc.tensor.transpose(p_turn[:, t, :], prob[a][:, g, t, :], ident[:])
+            w_b[a, g] = sb.tile([P, P, PACK], BF16, name="w_b%d%d" % (a, g), align_bytes=64)
+            scale = vs_col[g][:].unsqueeze(1).broadcast_to([P, P, PACK])
+            nc.vector.tensor_tensor(w_b[a, g][:], p_turn[:].rearrange("s t q -> s q t"), scale, ALU.mult)
 
-        def quant(a, g):
+        def quantise(a, g):
             w_codes[a, g] = sb.tile([P, P], U32, name="w_codes%d%d" % (a, g), align_bytes=64)
             w_scales[a, g] = sb.tile([P, P], U8, name="w_scales%d%d" % (a, g), align_bytes=64)
             nc.vector.quantize_mx(w_codes[a, g][:].bitcast(FP8X4), w_scales[a, g][:], w_b[a, g][:].rearrange("s q t -> s (q t)"))
 
-        def finish(a, cols, tag, on_vector):
+        def multiply(a, cols, bank):
             width = cols.stop - cols.start
-            y = ps.tile([P, width], F32, name="y", tag=tag)
-            for g in range(2):
+            y = ps.tile([P, width], F32, name="y", tag=bank)
+            for g in range(PASSES):
                 nc.tensor.matmul_mx(
                     y[:],
                     lhsT=w_codes[a, g][:].bitcast(FP8X4),
@@ -152,24 +178,25 @@ def tile_attend_cap_topk_kernel(tc, qT, k_words, k_scales, vT, vs, offs, out):
                     rhs=v_codes[:, g, cols].bitcast(FP8X4),
                     rhs_scale=v_scales[:, g, cols],
                     start=(g == 0),
-                    stop=(g == 1),
+                    stop=(g == PASSES - 1),
                 )
-            res = sb.tile([P, width], F32, name="res" + tag)
-            if on_vector:
-                nc.vector.tensor_scalar(res[:], y[:], inv[:, a : a + 1], None, ALU.mult)
-                nc.sync.dma_start(out[0, a * P : (a + 1) * P, cols], res[:])
-            else:
-                nc.scalar.activation(res[:], y[:], ACT.Copy, scale=inv[:, a : a + 1])
-                (nc.sync, nc.scalar)[a].dma_start(out[0, a * P : (a + 1) * P, cols], res[:])
+            res = sb.tile([P, width], F32, name="res_" + bank)
+            return y, res
 
         weigh(0, 0)
         weigh(0, 1)
-        quant(0, 0)
+        quantise(0, 0)
         weigh(1, 0)
-        quant(0, 1)
-        finish(0, slice(0, DV), "y0", False)
+        quantise(0, 1)
+        y, res = multiply(0, slice(0, DV), "y0")
+        nc.scalar.activation(res[:], y[:], ACT.Copy, scale=inv[:, 0:1])
+        nc.sync.dma_start(out[0, 0:P, :], res[:])
         weigh(1, 1)
-        quant(1, 0)
-        quant(1, 1)
-        finish(1, slice(0, P), "y1", False)
-        finish(1, slice(P, DV), "main2", True)
+        quantise(1, 0)
+        quantise(1, 1)
+        y, res = multiply(1, slice(0, P), "y1")
+        nc.scalar.activation(res[:], y[:], ACT.Copy, scale=inv[:, 1:2])
+        nc.scalar.dma_start(out[0, P:NQ, 0:P], res[:])
+        y, res = multiply(1, slice(P, DV), "score2")
+        nc.vector.tensor_scalar(res[:], y[:], inv[:, 1:2], None, ALU.mult)
+        nc.sync.dma_start(out[0, P:NQ, P:DV], res[:])

from contextlib import ExitStack

import concourse.mybir as mybir
from concourse.masks import make_identity

F32 = mybir.dt.float32
BF16 = mybir.dt.bfloat16
I32 = mybir.dt.int32
U32 = mybir.dt.uint32
U16 = mybir.dt.uint16
U8 = mybir.dt.uint8
FP8X4 = mybir.dt.float8_e4m3fn_x4
ACT = mybir.ActivationFunctionType
ALU = mybir.AluOpType

P = 128
PACK = 4
PASS = P * PACK
T, N, D, DV, NQ = 2048, 1024, 512, 256, 256
PASSES = N // PASS
Q_TILES = NQ // P
LIST_COLS = PASS // 16
QUADRANT = 32
CAP = 2.0

FLOPS = 2 * NQ * N * (D + DV)
BYTES = 4 * D * NQ + D * T + (D // 32) * T + 4 * DV * T + 4 * T + 2 * P * N // 16 + 4 * NQ * DV


def tile_attend_cap_topk_kernel(tc, qT, k_words, k_scales, vT, vs, offs, out):
    nc = tc.nc
    with ExitStack() as ctx:
        sb = ctx.enter_context(tc.tile_pool(name="sb", bufs=1))
        ps = ctx.enter_context(tc.psum_pool(name="ps", bufs=1))


        offsets = sb.tile([P, N // 16], U16, name="offsets")
        ks_pool = sb.tile([P, T], U8, name="ks_pool", align_bytes=64)
        kw_pool = sb.tile([P, T], U32, name="kw_pool", align_bytes=64)
        vs_pool = sb.tile([P, T], F32, name="vs_pool", align_bytes=64)
        q_raw = sb.tile([P, PACK, NQ], F32, name="q_raw", align_bytes=64)
        v0_raw = [sb.tile([P, T // 2], F32, name="v0_raw%d" % c, align_bytes=64) for c in range(2)]
        v0_pool = sb.tile([P, T], BF16, name="v0_pool", align_bytes=64)
        v1_pool = sb.tile([P, T], F32, name="v1_pool", tag="v1_pool", align_bytes=64)
        ident = sb.tile([P, P], F32, name="ident", align_bytes=64)

        nc.vector.memset(vs_pool[:, 0 : T // 2], 0.0)
        nc.gpsimd.memset(vs_pool[:, T // 2 : T], 0.0)
        make_identity(nc, ident[:])

        for quad in range(P // QUADRANT):
            rows = k_scales[0:1, 4 * quad : 4 * quad + 4, :].bitcast(I32)
            nc.sync.dma_start(
                ks_pool[QUADRANT * quad : QUADRANT * (quad + 1), :].bitcast(I32),
                rows.broadcast_to([QUADRANT // 4, 4, T // 4]),
            )
        nc.sync.dma_start(offsets[:], offs)
        nc.sync.dma_start(q_raw[:], qT[0].rearrange("(p j) q -> p j q", j=PACK))
        nc.sync.dma_start(vs_pool[0:1, :], vs[0:1, :])
        for c in range(2):
            nc.sync.dma_start(v0_raw[c][:], vT[0:P, c * (T // 2) : (c + 1) * (T // 2)])
        nc.sync.dma_start(kw_pool[:].bitcast(I32), k_words[0].rearrange("p t r -> p (t r)").bitcast(I32))
        nc.sync.dma_start(v1_pool[:], vT[P : 2 * P, :])

        q_b = sb.tile([P, NQ, PACK], BF16, name="q_b", align_bytes=64)
        nc.scalar.activation(q_b[:], q_raw[:].rearrange("p j q -> p q j"), ACT.Copy)
        q_codes = sb.tile([P, NQ], U32, name="q_codes", align_bytes=64)
        q_scales = sb.tile([P, NQ], U8, name="q_scales", align_bytes=64)

        ks_g = sb.tile([P, N], U8, name="ks_g", align_bytes=64)
        kw_g = sb.tile([P, N], U32, name="kw_g", align_bytes=64)
        vs_g = sb.tile([P, N], F32, name="vs_g", align_bytes=64)
        v_g = [sb.tile([P, N], BF16, name="v_g%d" % e, align_bytes=64) for e in range(DV // P)]

        def slots(g):
            return slice(PASS * g, PASS * (g + 1))

        def entries(g):
            return offsets[:, LIST_COLS * g : LIST_COLS * (g + 1)]

        nc.vector.tensor_copy(ks_g[:], ks_pool[:].indirect(offsets[:]))
        nc.vector.tensor_copy(vs_g[:], vs_pool[:].indirect(offsets[:]))
        nc.vector.quantize_mx(q_codes[:].bitcast(FP8X4), q_scales[:], q_b[:].rearrange("p q j -> p (q j)"))
        for g in range(PASSES):
            nc.vector.tensor_copy(kw_g[:, slots(g)], kw_pool[:].indirect(entries(g)))

        for c in range(2):
            nc.scalar.activation(v0_pool[:, c * (T // 2) : (c + 1) * (T // 2)], v0_raw[c][:], ACT.Copy)
        nc.scalar.activation(v_g[0][:], v0_pool[:].indirect(offsets[:]), ACT.Copy)

        vs_col = [sb.tile([P, PACK], F32, name="vs_col%d" % g) for g in range(PASSES)]
        for g in range(PASSES):
            nc.sync.dma_start(vs_col[g][:], vs_g[0:1, slots(g)])

        th = [sb.tile([P, PASSES, PACK, P], F32, name="th%d" % a, tag="th%d" % a, align_bytes=64) for a in range(Q_TILES)]
        for a in range(Q_TILES):
            for g in range(PASSES):
                score = ps.tile([P, PASS], F32, name="score", tag="score%d" % (PASSES * a + g))
                nc.tensor.matmul_mx(
                    score[:],
                    lhsT=q_codes[:, a * P : (a + 1) * P].bitcast(FP8X4),
                    lhsT_scale=q_scales[:, a * P : (a + 1) * P],
                    rhs=kw_g[:, slots(g)].bitcast(FP8X4),
                    rhs_scale=ks_g[:, slots(g)],
                    start=True,
                    stop=True,
                )
                nc.scalar.activation(th[a][:, g, :, :], score[:].rearrange("q (s t) -> q t s", t=PACK), ACT.Tanh, scale=1.0 / CAP)

        for g in range(PASSES):
            nc.vector.tensor_copy(v_g[1][:, slots(g)], v1_pool[:].indirect(entries(g)))

        neg_c = sb.tile([P, Q_TILES, N], F32, name="neg_c", tag="v1_pool", align_bytes=64)
        neg_m = [sb.tile([P, 1], F32, name="neg_m%d" % a) for a in range(Q_TILES)]
        prob = [sb.tile([P, PASSES, PACK, P], F32, name="prob%d" % a) for a in range(Q_TILES)]
        part = sb.tile([P, Q_TILES, PASSES], F32, name="part")
        total = sb.tile([P, Q_TILES], F32, name="total")
        for a in range(Q_TILES):
            nc.vector.tensor_scalar(
                neg_c[:, a, :], th[a][:].rearrange("q g t s -> q (g t s)"), -CAP, None, ALU.mult, ALU.min, accum_out=neg_m[a][:]
            )
            for g in range(PASSES):
                nc.scalar.activation(
                    prob[a][:, g, :, :].rearrange("q t s -> q (t s)"),
                    neg_c[:, a, slots(g)],
                    ACT.Exp,
                    bias=neg_m[a][:],
                    scale=-1.0,
                    accum_out=part[:, a, g : g + 1],
                )

        v_b = sb.tile([P, PASSES, DV, PACK], BF16, name="v_b", align_bytes=64)
        v_words = v_b[:].rearrange("s g e t -> s (g e t)").bitcast(F32).rearrange("s (g e u) -> s g e u", g=PASSES, u=2)
        for e, passes, bank in ((0, (0, 1), "score2"), (1, (0,), "score3"), (1, (1,), "y1")):
            words = v_g[e][:].bitcast(F32)
            v_turn = ps.tile([P, len(passes), 2, P], F32, name="v_turn", tag=bank)
            for n, g in enumerate(passes):
                for u in range(2):
                    nc.tensor.transpose(v_turn[:, n, u, :], words[:, PASS // 2 * g + u : PASS // 2 * (g + 1) : 2], ident[:])
            nc.scalar.copy(v_words[:, passes[0] : passes[-1] + 1, e * P : (e + 1) * P, :], v_turn[:].rearrange("s g u e -> s g e u"))
        v_codes = sb.tile([P, PASSES, DV], U32, name="v_codes", tag="th1", align_bytes=64)
        v_scales = sb.tile([P, PASSES, DV], U8, name="v_scales", align_bytes=64)
        nc.vector.quantize_mx(
            v_codes[:].rearrange("s g e -> s (g e)").bitcast(FP8X4),
            v_scales[:].rearrange("s g e -> s (g e)"),
            v_b[:].rearrange("s g e t -> s (g e t)"),
        )

        inv = sb.tile([P, Q_TILES], F32, name="inv")
        nc.gpsimd.tensor_tensor(total[:], part[:, :, 0], part[:, :, 1], ALU.add)
        nc.vector.reciprocal(inv[:], total[:])

        w_b = {}
        w_codes = {}
        w_scales = {}

        def weigh(a, g):
            p_turn = ps.tile([P, PACK, P], F32, name="p_turn", tag=("score%d", "turn%d")[a] % g)
            for t in range(PACK):
                nc.tensor.transpose(p_turn[:, t, :], prob[a][:, g, t, :], ident[:])
            w_b[a, g] = sb.tile([P, P, PACK], BF16, name="w_b%d%d" % (a, g), align_bytes=64)
            scale = vs_col[g][:].unsqueeze(1).broadcast_to([P, P, PACK])
            nc.vector.tensor_tensor(w_b[a, g][:], p_turn[:].rearrange("s t q -> s q t"), scale, ALU.mult)

        def quantise(a, g):
            w_codes[a, g] = sb.tile([P, P], U32, name="w_codes%d%d" % (a, g), align_bytes=64)
            w_scales[a, g] = sb.tile([P, P], U8, name="w_scales%d%d" % (a, g), align_bytes=64)
            nc.vector.quantize_mx(w_codes[a, g][:].bitcast(FP8X4), w_scales[a, g][:], w_b[a, g][:].rearrange("s q t -> s (q t)"))

        def multiply(a, cols, bank):
            width = cols.stop - cols.start
            y = ps.tile([P, width], F32, name="y", tag=bank)
            for g in range(PASSES):
                nc.tensor.matmul_mx(
                    y[:],
                    lhsT=w_codes[a, g][:].bitcast(FP8X4),
                    lhsT_scale=w_scales[a, g][:],
                    rhs=v_codes[:, g, cols].bitcast(FP8X4),
                    rhs_scale=v_scales[:, g, cols],
                    start=(g == 0),
                    stop=(g == PASSES - 1),
                )
            res = sb.tile([P, width], F32, name="res_" + bank)
            return y, res

        weigh(0, 0)
        weigh(0, 1)
        quantise(0, 0)
        weigh(1, 0)
        quantise(0, 1)
        y, res = multiply(0, slice(0, DV), "y0")
        nc.scalar.activation(res[:], y[:], ACT.Copy, scale=inv[:, 0:1])
        nc.sync.dma_start(out[0, 0:P, :], res[:])
        weigh(1, 1)
        quantise(1, 0)
        quantise(1, 1)
        y, res = multiply(1, slice(0, P), "y1")
        nc.scalar.activation(res[:], y[:], ACT.Copy, scale=inv[:, 1:2])
        nc.scalar.dma_start(out[0, P:NQ, 0:P], res[:])
        y, res = multiply(1, slice(P, DV), "score2")
        nc.vector.tensor_scalar(res[:], y[:], inv[:, 1:2], None, ALU.mult)
        nc.sync.dma_start(out[0, P:NQ, P:DV], res[:])
